import numpy as np
import ml_dtypes


def mxq(x, axis, fmt="e4m3"):
    dtype, down = {"e4m3": (ml_dtypes.float8_e4m3fn, 7), "e5m2": (ml_dtypes.float8_e5m2, 14)}[fmt]
    v = np.moveaxis(np.asarray(x, np.float32).astype(ml_dtypes.bfloat16).astype(np.float64), axis, -1)
    blocks = v.reshape(v.shape[:-1] + (-1, 32))
    amax = np.abs(blocks).max(-1, keepdims=True)
    byte = np.maximum(np.where(amax > 0, np.frexp(amax)[1] - 1 + 127, 0) - down, 1)
    scale = np.exp2(byte - 127.0)
    codes = (blocks / scale).astype(np.float32).astype(dtype).astype(np.float64)
    return np.moveaxis((codes * scale).reshape(v.shape), -1, axis)


WIDE = False


def mx_kscale(k):
    if not WIDE:
        return np.ones(k)
    levels = np.array([30, -30])
    if k % 512:
        return np.exp2(np.random.permutation(np.resize(levels, k // 32))).repeat(32)
    a = np.empty((k // 512, 16))
    for p in range(k // 512):
        a[p, :8] = np.random.permutation(np.resize(levels, 8))
        for g in range(8):
            far = levels[np.abs(levels - a[p, g]) >= 10]
            a[p, g + 8] = far[np.random.randint(len(far))]
    return np.exp2(a.ravel()).repeat(32)


def f64(x):
    return np.asarray(x).astype(np.float64)


def striped(idx):
    return np.tile(np.asarray(idx).reshape(-1, 16).T, (8, 1)).astype(np.uint16)


def unstriped(offs):
    return offs[:16].T.reshape(-1).astype(np.int64)


def striped8(idx):
    return np.asarray(idx).reshape(8, -1, 16).transpose(0, 2, 1).reshape(128, -1).astype(np.uint16)


def unstriped8(offs):
    return offs.reshape(8, 16, -1).transpose(0, 2, 1).reshape(8, -1).astype(np.int64)


def pick8(x, idx, run):
    r = np.arange(len(x))
    return x[r[:, None], idx[r % (8 * run) // run]]


E2M1 = np.array([0.0, 0.5, 1.0, 1.5, 2.0, 3.0, 4.0, 6.0, -0.0, -0.5, -1.0, -1.5, -2.0, -3.0, -4.0, -6.0])


def pack_weight(w, fmt):
    k, n = w.shape
    w = f64(np.asarray(w, np.float32).astype(ml_dtypes.bfloat16)).reshape(k // 32, 32, n)
    amax = np.abs(w).max(1)
    if fmt in ("e4m3", "e5m2"):
        byte = np.frexp(amax)[1] - 1 + 127 - (7 if fmt == "e4m3" else 14)
    else:
        mant, ex = np.frexp(amax / 6.0)
        byte = np.where(mant > 0.5, ex, ex - 1) + 127
    byte = np.clip(np.where(amax > 0, byte, 1), 1, 254)
    scaled = (w * np.exp2(127.0 - byte)[:, None, :]).reshape(k, n).astype(np.float32)
    by_word = np.ascontiguousarray(scaled.reshape(k // 512, 128, 4, n).transpose(0, 1, 3, 2))
    if fmt in ("e4m3", "e5m2"):
        words = by_word.astype(ml_dtypes.float8_e4m3fn if fmt == "e4m3" else ml_dtypes.float8_e5m2).view(np.uint8)
    else:
        c = by_word.astype(ml_dtypes.float4_e2m1fn).view(np.uint8) & 0xF
        words = (c[..., 0::2] | (c[..., 1::2] << 4)).reshape(k // 512, 128, 2 * n)
    return np.ascontiguousarray(words), np.ascontiguousarray(byte.astype(np.uint8).reshape(k // 512, 16, n))


def unpack_weight(words, scales, fmt):
    g, _, n = scales.shape
    words = np.ascontiguousarray(words).reshape(g, 128, n, -1)
    if fmt in ("e4m3", "e5m2"):
        vals = words.view(ml_dtypes.float8_e4m3fn if fmt == "e4m3" else ml_dtypes.float8_e5m2).astype(np.float64)
    else:
        nib = np.empty((g, 128, n, 4), np.uint8)
        nib[..., 0::2] = words & 0xF
        nib[..., 1::2] = words >> 4
        vals = E2M1[nib]
    vals = vals * np.repeat(np.exp2(scales.astype(np.float64) - 127.0), 8, axis=1)[..., None]
    return vals.transpose(0, 1, 3, 2).reshape(g * 512, n)


K, T, J, R, F, Z, M, Q, O, D, N, U = 512, 1024, 256, 512, 512, 1024, 512, 128, 128, 256, 256, 128


def setup_inputs():
    n = np.random.standard_normal
    idx = np.random.permutation(T)[:J]
    idx2 = np.random.permutation(Z)[:J]
    idx3 = np.stack([np.random.permutation(J)[:O] for _ in range(8)])
    idx4 = np.stack([np.random.permutation(J)[:O] for _ in range(8)])
    idx5 = np.random.permutation(T)[:D]
    idx6 = np.random.permutation(D)[:U]
    idx7 = np.random.permutation(D)[:U]
    fk = mx_kscale(K)
    ff = mx_kscale(F)
    fm = mx_kscale(M)
    fr = mx_kscale(R)
    xtp = pack_weight(n((K, T)) / fk[:, None], "e2m1")
    xop = pack_weight(n((F, Z)) / ff[:, None], "e4m3")
    wp = pack_weight(n((K, R)) * 1 / np.sqrt(K) * fk[:, None], "e4m3")
    w0p = pack_weight(n((F, R)) * 1 / np.sqrt(F) * ff[:, None], "e2m1")
    xcp = pack_weight(n((M, Q)) / fm[:, None], "e4m3")
    wgp = pack_weight(n((M, R)) * 1 / np.sqrt(M) * fm[:, None] * fr, "e5m2")
    wbp = pack_weight(n((R, N)) * 1 / np.sqrt(R) / fr[:, None], "e2m1")
    wsp = pack_weight(n((K, N)) * 1 / np.sqrt(K) * fk[:, None], "e4m3")
    return {
        "xt_words": xtp[0],
        "xt_scales": xtp[1],
        "xo_words": xop[0],
        "xo_scales": xop[1],
        "w_words": wp[0],
        "w_scales": wp[1],
        "w0_words": w0p[0],
        "w0_scales": w0p[1],
        "xc_words": xcp[0],
        "xc_scales": xcp[1],
        "wg_words": wgp[0],
        "wg_scales": wgp[1],
        "wb_words": wbp[0],
        "wb_scales": wbp[1],
        "ws_words": wsp[0],
        "ws_scales": wsp[1],
        "so": (np.random.uniform(0.5, 1.6, (N, 1))).astype(np.float32),
        "sp": (np.random.uniform(0.5, 1.6, (N, 1))).astype(np.float32),
        "offs": striped(idx),
        "offs2": striped(idx2),
        "offs3": striped8(idx3),
        "offs4": striped8(idx4),
        "offs5": striped(idx5),
        "offs6": striped(idx6),
        "offs7": striped(idx7),
    }


def reference(xt_words, xt_scales, xo_words, xo_scales, w_words, w_scales, w0_words, w0_scales, xc_words, xc_scales, wg_words, wg_scales, wb_words, wb_scales, ws_words, ws_scales, so, sp, offs, offs2, offs3, offs4, offs5, offs6, offs7):
    idx = unstriped(offs)
    idx2 = unstriped(offs2)
    idx3 = unstriped8(offs3)
    idx4 = unstriped8(offs4)
    idx5 = unstriped(offs5)
    idx6 = unstriped(offs6)
    idx7 = unstriped(offs7)
    xtu = unpack_weight(xt_words, xt_scales, "e2m1")
    xou = unpack_weight(xo_words, xo_scales, "e4m3")
    wu = unpack_weight(w_words, w_scales, "e4m3")
    w0u = unpack_weight(w0_words, w0_scales, "e2m1")
    xcu = unpack_weight(xc_words, xc_scales, "e4m3")
    wgu = unpack_weight(wg_words, wg_scales, "e5m2")
    wbu = unpack_weight(wb_words, wb_scales, "e2m1")
    wsu = unpack_weight(ws_words, ws_scales, "e4m3")
    xtidxg = xtu[:, idx]
    xoidx2g = xou[:, idx2]
    a = wu.T @ xtidxg + w0u.T @ xoidx2g
    g0 = wgu.T @ xcu
    ga = g0[:, 0:1]
    gb = g0[:, 64:65]
    h1 = np.maximum(pick8(a, idx3, 64) * ga, pick8(a, idx4, 64) * gb)
    hid = np.concatenate([h1, g0], axis=1)
    hidq = mxq(hid, 0, "e5m2")
    xtidx5g = xtu[:, idx5]
    p = wbu.T @ hidq + wsu.T @ xtidx5g
    y = np.maximum(p[:, idx6] * f64(so), p[:, idx7] * f64(sp))
    return y

@@ -1,0 +1,226 @@
+from contextlib import ExitStack
+
+import concourse.mybir as mybir
+
+F32 = mybir.dt.float32
+BF16 = mybir.dt.bfloat16
+I32 = mybir.dt.int32
+U32 = mybir.dt.uint32
+U16 = mybir.dt.uint16
+U8 = mybir.dt.uint8
+E4M3 = mybir.dt.float8_e4m3fn_x4
+E5M2 = mybir.dt.float8_e5m2_x4
+E2M1 = mybir.dt.float4_e2m1fn_x4
+COPY = mybir.ActivationFunctionType.Copy
+MAX = mybir.AluOpType.max
+
+P = 128
+PACK = 4
+T, J, R, Z, Q, O, D, N, U = 1024, 256, 512, 1024, 128, 128, 256, 256, 128
+K = 512
+FLOPS = 2 * K * (2 * R * J + R * Q + 2 * N * D)
+
+
+def tile_list_ctxgroups_bank_further_pairweighed_kernel(
+    tc, xt_words, xt_scales, xo_words, xo_scales, w_words, w_scales, w0_words, w0_scales,
+    xc_words, xc_scales, wg_words, wg_scales, wb_words, wb_scales, ws_words, ws_scales,
+    so, sp, offs, offs2, offs3, offs4, offs5, offs6, offs7, out,
+):
+    nc = tc.nc
+    with ExitStack() as ctx:
+        sb = ctx.enter_context(tc.tile_pool(name="sb", bufs=1))
+        ps = ctx.enter_context(tc.psum_pool(name="ps", bufs=1))
+
+        def tile(name, shape, dtype):
+            return sb.tile(shape, dtype, name=name, align_bytes=64)
+
+        def load_list(name, src):
+            dst = tile(name, list(src.shape), U16)
+            nc.sync.dma_start(dst[:], src)
+            return dst
+
+        def load_words(queue, name, src, dtype):
+            rows = src[0] if src.ndim == 3 else src[0].rearrange("p c t -> p (c t)")
+            width = rows.shape[1] // (4 if dtype == U32 else 2)
+            dst = tile(name, [P, width], dtype)
+            queue.dma_start(dst[:].bitcast(I32), rows.bitcast(I32))
+            return dst
+
+        def load_rows(queue, dst, src, col):
+            rows = src[0].bitcast(I32).rearrange("(q r) c -> r q c", r=4)
+            queue.dma_start(dst[:, :, col : col + rows.shape[2]], rows)
+
+        def load_half(queue, dst, src, col, h):
+            rows = src[0].bitcast(I32).rearrange("(b h r) c -> h r b c", b=2, h=2)
+            queue.dma_start(dst[32 * h : 32 * h + 4, :, col : col + rows.shape[3]], rows[h])
+
+        def load_quad(queue, dst, src, col, quad):
+            rows = src[0, 4 * quad : 4 * quad + 4, :].bitcast(I32)
+            queue.dma_start(dst[32 * quad : 32 * quad + 4, col : col + rows.shape[1]], rows)
+
+        so_t = tile("so_t", [P, 2], F32)
+        sp_t = tile("sp_t", [P, 2], F32)
+
+        def load_weight(queue, dst, src):
+            with nc.allow_non_contiguous_dma(reason="one weight a partition"):
+                queue.dma_start(dst[:], src.rearrange("(i p) o -> p (i o)", p=P))
+
+        def gather(name, window, offsets, dtype):
+            dst = tile(name, [P, J], dtype)
+            nc.vector.tensor_copy(dst[:], window.indirect(offsets[:]))
+            return dst
+
+        def deal_words(copy, name, src, dtype):
+            dst = tile(name, [P, R], dtype)
+            copy(
+                dst[:].rearrange("p (t b i) -> p b t i", t=PACK, i=4),
+                src[:].rearrange("p (b i t) -> p b t i", t=PACK, i=4),
+            )
+            return dst
+
+        def deal_scales(engine, name, src):
+            dst = tile(name, [P, R], U8)
+            engine.tensor_copy(dst[:].rearrange("p (t m) -> p t m", t=PACK), src.rearrange("p (m t) -> p t m", t=PACK))
+            return dst
+
+        W_p = tile("W_p", [P, 1664], U8)
+        nc.vector.memset(W_p[:].bitcast(I32), 0)
+        W_st = tile("W_st", [4, 4, 416], I32)
+        xt_p = tile("xt_p", [P, 1024], U8)
+        nc.vector.memset(xt_p[:].bitcast(I32), 0)
+        xt_st = tile("xt_st", [4, 4, 256], I32)
+        xo_p = tile("xo_p", [P, 1024], U8)
+        nc.vector.memset(xo_p[:].bitcast(I32), 0)
+        xo_st = tile("xo_st", [4, 4, 256], I32)
+        B_p = tile("B_p", [P, 512], U8)
+        nc.vector.memset(B_p[:].bitcast(I32), 0)
+        load_rows(nc.sync, W_st, w_scales, 0)
+        load_rows(nc.sync, W_st, wg_scales, 128)
+        load_rows(nc.sync, W_st, w0_scales, 256)
+        load_rows(nc.sync, W_st, xc_scales, 384)
+        load_rows(nc.sync, xt_st, xt_scales, 0)
+        l1 = load_list("l1", offs)
+        xt_w = load_words(nc.sync, "xt_w", xt_words, U16)
+        xo_w = load_words(nc.sync, "xo_w", xo_words, U32)
+        w_w = load_words(nc.sync, "w_w", w_words, U32)
+        load_rows(nc.sync, xo_st, xo_scales, 0)
+        l2 = load_list("l2", offs2)
+        wg_w = load_words(nc.sync, "wg_w", wg_words, U32)
+        w0_w = load_words(nc.sync, "w0_w", w0_words, U16)
+        xc_w = load_words(nc.sync, "xc_w", xc_words, U32)
+        l3 = load_list("l3", offs3)
+        l4 = load_list("l4", offs4)
+        l5 = load_list("l5", offs5)
+        ws_w = load_words(nc.sync, "ws_w", ws_words, U32)
+        load_quad(nc.sync, B_p[:].bitcast(I32), ws_scales, 0, 0)
+        load_quad(nc.sync, B_p[:].bitcast(I32), ws_scales, 0, 1)
+        load_quad(nc.sync, B_p[:].bitcast(I32), ws_scales, 0, 2)
+        load_quad(nc.sync, B_p[:].bitcast(I32), ws_scales, 0, 3)
+        wb_w = load_words(nc.sync, "wb_w", wb_words, U16)
+        load_quad(nc.sync, B_p[:].bitcast(I32), wb_scales, 64, 0)
+        load_quad(nc.sync, B_p[:].bitcast(I32), wb_scales, 64, 1)
+        load_quad(nc.sync, B_p[:].bitcast(I32), wb_scales, 64, 2)
+        load_quad(nc.sync, B_p[:].bitcast(I32), wb_scales, 64, 3)
+        l6 = load_list("l6", offs6)
+        l7 = load_list("l7", offs7)
+        load_weight(nc.sync, so_t, so)
+        load_weight(nc.sync, sp_t, sp)
+        for quad in range(4):
+            nc.vector.tensor_copy(W_p[32 * quad : 32 * quad + 4, :].bitcast(I32), W_st[:, quad, :])
+        for quad in range(4):
+            nc.vector.tensor_copy(xt_p[32 * quad : 32 * quad + 4, :].bitcast(I32), xt_st[:, quad, :])
+        w_sd = deal_scales(nc.gpsimd, "w_sd", W_p[:, 0:512])
+        wg_sd = deal_scales(nc.gpsimd, "wg_sd", W_p[:, 512:1024])
+        w0_sd = deal_scales(nc.gpsimd, "w0_sd", W_p[:, 1024:1536])
+        xt1_w = gather("xt1_w", xt_w[:], l1, U16)
+        xt1_s = gather("xt1_s", xt_p[:], l1, U8)
+        for quad in range(4):
+            nc.vector.tensor_copy(xo_p[32 * quad : 32 * quad + 4, :].bitcast(I32), xo_st[:, quad, :])
+        xo2_w = gather("xo2_w", xo_w[:], l2, U32)
+        xo2_s = gather("xo2_s", xo_p[:], l2, U8)
+        w_wd = deal_words(nc.scalar.copy, "w_wd", w_w, U32)
+        wg_wd = deal_words(nc.scalar.copy, "wg_wd", wg_w, U32)
+        w0_wd = deal_words(nc.scalar.copy, "w0_wd", w0_w, U16)
+        xc_s = W_p[:, 1536:1664]
+        ws_s = B_p[:, 0:256]
+        wb_s = B_p[:, 256:512]
+
+        a_ps = [ps.tile([P, J], F32, name="a_ps%d" % t) for t in range(PACK)]
+        g_ps = ps.tile([P, PACK, Q], F32, name="g_ps")
+        for t in range(PACK):
+            cols = slice(P * t, P * (t + 1))
+            nc.tensor.matmul_mx(a_ps[t][:], lhsT=w_wd[:, cols].bitcast(E4M3), lhsT_scale=w_sd[:, cols],
+                                rhs=xt1_w[:].bitcast(E2M1), rhs_scale=xt1_s[:], start=True, stop=False)
+        for t in range(PACK):
+            cols = slice(P * t, P * (t + 1))
+            nc.tensor.matmul_mx(g_ps[:, t, :], lhsT=wg_wd[:, cols].bitcast(E5M2), lhsT_scale=wg_sd[:, cols],
+                                rhs=xc_w[:].bitcast(E4M3), rhs_scale=xc_s, start=True, stop=True)
+        for t in range(PACK):
+            cols = slice(P * t, P * (t + 1))
+            nc.tensor.matmul_mx(a_ps[t][:], lhsT=w0_wd[:, cols].bitcast(E2M1), lhsT_scale=w0_sd[:, cols],
+                                rhs=xo2_w[:].bitcast(E4M3), rhs_scale=xo2_s[:], start=False, stop=True)
+
+        gains = tile("gains", [P, PACK, 2], F32)
+        nc.scalar.copy(gains[:], g_ps[:, :, 0:Q:64])
+        hid_g = tile("hid_g", [P, Q, PACK], BF16)
+        hid_h = tile("hid_h", [P, O, PACK], BF16)
+        y3 = tile("y3", [P, PACK, O], F32)
+        y4 = tile("y4", [P, PACK, O], F32)
+        a_sb = [tile("a_sb%d" % t, [P, J], F32) for t in range(PACK)]
+
+        def quantise(name, src):
+            codes = tile(name + "_w", [P, P], U32)
+            scales = tile(name + "_s", [P, P], U8)
+            nc.vector.quantize_mx(out=codes[:].bitcast(E5M2), scales=scales[:], in_=src[:].rearrange("p c t -> p (c t)"))
+            return codes, scales
+
+        def larger(pair):
+            nc.vector.tensor_tensor(hid_h[:, :, pair], y3[:, pair, :].rearrange("p t c -> p c t"),
+                                    y4[:, pair, :].rearrange("p t c -> p c t"), MAX)
+
+        for t in range(PACK):
+            nc.vector.tensor_copy(a_sb[t][:], a_ps[t][:])
+        for t in range(PACK):
+            nc.scalar.activation(y3[:, t, :], a_sb[t][:].indirect(l3[:]), COPY, scale=gains[:, t, 0:1])
+            nc.scalar.activation(y4[:, t, :], a_sb[t][:].indirect(l4[:]), COPY, scale=gains[:, t, 1:2])
+        nc.vector.tensor_copy(hid_g[:], g_ps[:].rearrange("p t c -> p c t"))
+        xt5_w = gather("xt5_w", xt_w[:], l5, U16)
+        hg_w, hg_s = quantise("hg", hid_g)
+        xt5_s = gather("xt5_s", xt_p[:], l5, U8)
+        larger(slice(0, 2))
+
+        pg_ps = ps.tile([P, 2, Q], F32, name="pg_ps")
+        ph_ps = [ps.tile([P, O], F32, name="ph_ps%d" % i) for i in range(2)]
+        p_sb = [tile("p_sb%d" % i, [P, D], F32) for i in range(2)]
+
+        def short_way(dst, i, places):
+            cols = slice(P * i, P * (i + 1))
+            nc.tensor.matmul_mx(dst, lhsT=ws_w[:, cols].bitcast(E4M3), lhsT_scale=ws_s[:, cols],
+                                rhs=xt5_w[:, places].bitcast(E2M1), rhs_scale=xt5_s[:, places], start=True, stop=False)
+
+        def output_matrix(dst, i, codes, scales):
+            cols = slice(P * i, P * (i + 1))
+            nc.tensor.matmul_mx(dst, lhsT=wb_w[:, cols].bitcast(E2M1), lhsT_scale=wb_s[:, cols],
+                                rhs=codes[:].bitcast(E5M2), rhs_scale=scales[:], start=False, stop=True)
+
+        for i in range(2):
+            short_way(pg_ps[:, i, :], i, slice(O, D))
+            output_matrix(pg_ps[:, i, :], i, hg_w, hg_s)
+        for i in range(2):
+            short_way(ph_ps[i][:], i, slice(0, O))
+        for i in range(2):
+            nc.vector.tensor_copy(p_sb[i][:, O:D], pg_ps[:, i, :])
+        larger(slice(2, 4))
+        hh_w, hh_s = quantise("hh", hid_h)
+        for i in range(2):
+            output_matrix(ph_ps[i][:], i, hh_w, hh_s)
+        for i in range(2):
+            nc.vector.tensor_copy(p_sb[i][:, 0:O], ph_ps[i][:])
+        for i in range(2):
+            y6 = tile("y6_%d" % i, [P, U], F32)
+            y7 = tile("y7_%d" % i, [P, U], F32)
+            res = tile("res%d" % i, [P, U], F32)
+            nc.scalar.activation(y6[:], p_sb[i][:].indirect(l6[:]), COPY, scale=so_t[:, i : i + 1])
+            nc.scalar.activation(y7[:], p_sb[i][:].indirect(l7[:]), COPY, scale=sp_t[:, i : i + 1])
+            nc.vector.tensor_tensor(res[:], y6[:], y7[:], MAX)
+            nc.sync.dma_start(out[P * i : P * (i + 1), :], res[:])

@@ -31,8 +31,8 @@ def tile_list_ctxgroups_bank_further_pairweighed_kernel(
         sb = ctx.enter_context(tc.tile_pool(name="sb", bufs=1))
         ps = ctx.enter_context(tc.psum_pool(name="ps", bufs=1))
 
-        def tile(name, shape, dtype):
-            return sb.tile(shape, dtype, name=name, align_bytes=64)
+        def tile(name, shape, dtype, tag=None):
+            return sb.tile(shape, dtype, name=name, tag=tag or name, align_bytes=64)
 
         def load_list(name, src):
             dst = tile(name, list(src.shape), U16)
@@ -65,8 +65,8 @@ def tile_list_ctxgroups_bank_further_pairweighed_kernel(
             with nc.allow_non_contiguous_dma(reason="one weight a partition"):
                 queue.dma_start(dst[:], src.rearrange("(i p) o -> p (i o)", p=P))
 
-        def gather(name, window, offsets, dtype):
-            dst = tile(name, [P, J], dtype)
+        def gather(name, window, offsets, dtype, tag=None):
+            dst = tile(name, [P, J], dtype, tag)
             nc.vector.tensor_copy(dst[:], window.indirect(offsets[:]))
             return dst
 
@@ -83,34 +83,38 @@ def tile_list_ctxgroups_bank_further_pairweighed_kernel(
             engine.tensor_copy(dst[:].rearrange("p (t m) -> p t m", t=PACK), src.rearrange("p (m t) -> p t m", t=PACK))
             return dst
 
+        xt_p = tile("xt_p", [P, 1024], U8)
+        nc.vector.memset(xt_p[:].bitcast(I32), 0)
+        xo_p = tile("xo_p", [P, 1024], U8)
+        nc.vector.memset(xo_p[:].bitcast(I32), 0)
         W_p = tile("W_p", [P, 1664], U8)
         nc.vector.memset(W_p[:].bitcast(I32), 0)
         W_st = tile("W_st", [4, 4, 416], I32)
-        xt_p = tile("xt_p", [P, 1024], U8)
-        nc.vector.memset(xt_p[:].bitcast(I32), 0)
-        xt_st = tile("xt_st", [4, 4, 256], I32)
-        xo_p = tile("xo_p", [P, 1024], U8)
-        nc.vector.memset(xo_p[:].bitcast(I32), 0)
-        xo_st = tile("xo_st", [4, 4, 256], I32)
         B_p = tile("B_p", [P, 512], U8)
         nc.vector.memset(B_p[:].bitcast(I32), 0)
-        load_rows(nc.sync, W_st, w_scales, 0)
-        load_rows(nc.sync, W_st, wg_scales, 128)
-        load_rows(nc.sync, W_st, w0_scales, 256)
         load_rows(nc.sync, W_st, xc_scales, 384)
-        load_rows(nc.sync, xt_st, xt_scales, 0)
+        load_rows(nc.scalar, W_st, w_scales, 0)
         l1 = load_list("l1", offs)
+        load_rows(nc.scalar, W_st, wg_scales, 128)
+        l2 = load_list("l2", offs2)
+        load_rows(nc.scalar, W_st, w0_scales, 256)
         xt_w = load_words(nc.sync, "xt_w", xt_words, U16)
         xo_w = load_words(nc.sync, "xo_w", xo_words, U32)
         w_w = load_words(nc.sync, "w_w", w_words, U32)
-        load_rows(nc.sync, xo_st, xo_scales, 0)
-        l2 = load_list("l2", offs2)
+        load_quad(nc.sync, xt_p[:].bitcast(I32), xt_scales, 0, 0)
+        load_quad(nc.sync, xt_p[:].bitcast(I32), xt_scales, 0, 1)
+        load_quad(nc.sync, xt_p[:].bitcast(I32), xt_scales, 0, 2)
+        load_quad(nc.sync, xt_p[:].bitcast(I32), xt_scales, 0, 3)
         wg_w = load_words(nc.sync, "wg_w", wg_words, U32)
         w0_w = load_words(nc.sync, "w0_w", w0_words, U16)
         xc_w = load_words(nc.sync, "xc_w", xc_words, U32)
+        load_quad(nc.sync, xo_p[:].bitcast(I32), xo_scales, 0, 0)
+        load_quad(nc.sync, xo_p[:].bitcast(I32), xo_scales, 0, 1)
+        load_quad(nc.sync, xo_p[:].bitcast(I32), xo_scales, 0, 2)
+        load_quad(nc.sync, xo_p[:].bitcast(I32), xo_scales, 0, 3)
+        l5 = load_list("l5", offs5)
         l3 = load_list("l3", offs3)
         l4 = load_list("l4", offs4)
-        l5 = load_list("l5", offs5)
         ws_w = load_words(nc.sync, "ws_w", ws_words, U32)
         load_quad(nc.sync, B_p[:].bitcast(I32), ws_scales, 0, 0)
         load_quad(nc.sync, B_p[:].bitcast(I32), ws_scales, 0, 1)
@@ -127,15 +131,11 @@ def tile_list_ctxgroups_bank_further_pairweighed_kernel(
         load_weight(nc.sync, sp_t, sp)
         for quad in range(4):
             nc.vector.tensor_copy(W_p[32 * quad : 32 * quad + 4, :].bitcast(I32), W_st[:, quad, :])
-        for quad in range(4):
-            nc.vector.tensor_copy(xt_p[32 * quad : 32 * quad + 4, :].bitcast(I32), xt_st[:, quad, :])
-        w_sd = deal_scales(nc.gpsimd, "w_sd", W_p[:, 0:512])
-        wg_sd = deal_scales(nc.gpsimd, "wg_sd", W_p[:, 512:1024])
-        w0_sd = deal_scales(nc.gpsimd, "w0_sd", W_p[:, 1024:1536])
         xt1_w = gather("xt1_w", xt_w[:], l1, U16)
+        w_sd = deal_scales(nc.vector, "w_sd", W_p[:, 0:512])
         xt1_s = gather("xt1_s", xt_p[:], l1, U8)
-        for quad in range(4):
-            nc.vector.tensor_copy(xo_p[32 * quad : 32 * quad + 4, :].bitcast(I32), xo_st[:, quad, :])
+        wg_sd = deal_scales(nc.vector, "wg_sd", W_p[:, 512:1024])
+        w0_sd = deal_scales(nc.vector, "w0_sd", W_p[:, 1024:1536])
         xo2_w = gather("xo2_w", xo_w[:], l2, U32)
         xo2_s = gather("xo2_s", xo_p[:], l2, U8)
         w_wd = deal_words(nc.scalar.copy, "w_wd", w_w, U32)
@@ -163,13 +163,14 @@ def tile_list_ctxgroups_bank_further_pairweighed_kernel(
         gains = tile("gains", [P, PACK, 2], F32)
         nc.scalar.copy(gains[:], g_ps[:, :, 0:Q:64])
         hid_g = tile("hid_g", [P, Q, PACK], BF16)
+        nc.scalar.copy(hid_g[:], g_ps[:].rearrange("p t c -> p c t"))
         hid_h = tile("hid_h", [P, O, PACK], BF16)
         y3 = tile("y3", [P, PACK, O], F32)
         y4 = tile("y4", [P, PACK, O], F32)
         a_sb = [tile("a_sb%d" % t, [P, J], F32) for t in range(PACK)]
 
-        def quantise(name, src):
-            codes = tile(name + "_w", [P, P], U32)
+        def quantise(name, src, tag=None):
+            codes = tile(name + "_w", [P, P], U32, tag)
             scales = tile(name + "_s", [P, P], U8)
             nc.vector.quantize_mx(out=codes[:].bitcast(E5M2), scales=scales[:], in_=src[:].rearrange("p c t -> p (c t)"))
             return codes, scales
@@ -183,10 +184,9 @@ def tile_list_ctxgroups_bank_further_pairweighed_kernel(
         for t in range(PACK):
             nc.scalar.activation(y3[:, t, :], a_sb[t][:].indirect(l3[:]), COPY, scale=gains[:, t, 0:1])
             nc.scalar.activation(y4[:, t, :], a_sb[t][:].indirect(l4[:]), COPY, scale=gains[:, t, 1:2])
-        nc.vector.tensor_copy(hid_g[:], g_ps[:].rearrange("p t c -> p c t"))
         xt5_w = gather("xt5_w", xt_w[:], l5, U16)
-        hg_w, hg_s = quantise("hg", hid_g)
-        xt5_s = gather("xt5_s", xt_p[:], l5, U8)
+        hg_w, hg_s = quantise("hg", hid_g, "w0_wd")
+        xt5_s = gather("xt5_s", xt_p[:], l5, U8, "w0_sd")
         larger(slice(0, 2))
 
         pg_ps = ps.tile([P, 2, Q], F32, name="pg_ps")

@@ -92,13 +92,13 @@ def tile_list_ctxgroups_bank_further_pairweighed_kernel(
         W_st = tile("W_st", [4, 4, 416], I32)
         B_p = tile("B_p", [P, 512], U8)
         nc.vector.memset(B_p[:].bitcast(I32), 0)
-        load_rows(nc.sync, W_st, xc_scales, 384)
-        load_rows(nc.scalar, W_st, w_scales, 0)
         l1 = load_list("l1", offs)
-        load_rows(nc.scalar, W_st, wg_scales, 128)
-        l2 = load_list("l2", offs2)
-        load_rows(nc.scalar, W_st, w0_scales, 256)
+        load_rows(nc.scalar, W_st, w_scales, 0)
         xt_w = load_words(nc.sync, "xt_w", xt_words, U16)
+        load_rows(nc.scalar, W_st, wg_scales, 128)
+        load_rows(nc.sync, W_st, xc_scales, 384)
+        load_rows(nc.scalar, W_st, w0_scales, 256)
+        l2 = load_list("l2", offs2)
         xo_w = load_words(nc.sync, "xo_w", xo_words, U32)
         w_w = load_words(nc.sync, "w_w", w_words, U32)
         load_quad(nc.sync, xt_p[:].bitcast(I32), xt_scales, 0, 0)
@@ -106,8 +106,8 @@ def tile_list_ctxgroups_bank_further_pairweighed_kernel(
         load_quad(nc.sync, xt_p[:].bitcast(I32), xt_scales, 0, 2)
         load_quad(nc.sync, xt_p[:].bitcast(I32), xt_scales, 0, 3)
         wg_w = load_words(nc.sync, "wg_w", wg_words, U32)
-        w0_w = load_words(nc.sync, "w0_w", w0_words, U16)
         xc_w = load_words(nc.sync, "xc_w", xc_words, U32)
+        w0_w = load_words(nc.sync, "w0_w", w0_words, U16)
         load_quad(nc.sync, xo_p[:].bitcast(I32), xo_scales, 0, 0)
         load_quad(nc.sync, xo_p[:].bitcast(I32), xo_scales, 0, 1)
         load_quad(nc.sync, xo_p[:].bitcast(I32), xo_scales, 0, 2)
@@ -129,12 +129,12 @@ def tile_list_ctxgroups_bank_further_pairweighed_kernel(
         l7 = load_list("l7", offs7)
         load_weight(nc.sync, so_t, so)
         load_weight(nc.sync, sp_t, sp)
+        xt1_w = gather("xt1_w", xt_w[:], l1, U16)
         for quad in range(4):
             nc.vector.tensor_copy(W_p[32 * quad : 32 * quad + 4, :].bitcast(I32), W_st[:, quad, :])
-        xt1_w = gather("xt1_w", xt_w[:], l1, U16)
         w_sd = deal_scales(nc.vector, "w_sd", W_p[:, 0:512])
-        xt1_s = gather("xt1_s", xt_p[:], l1, U8)
         wg_sd = deal_scales(nc.vector, "wg_sd", W_p[:, 512:1024])
+        xt1_s = gather("xt1_s", xt_p[:], l1, U8)
         w0_sd = deal_scales(nc.vector, "w0_sd", W_p[:, 1024:1536])
         xo2_w = gather("xo2_w", xo_w[:], l2, U32)
         xo2_s = gather("xo2_s", xo_p[:], l2, U8)
@@ -149,20 +149,18 @@ def tile_list_ctxgroups_bank_further_pairweighed_kernel(
         g_ps = ps.tile([P, PACK, Q], F32, name="g_ps")
         for t in range(PACK):
             cols = slice(P * t, P * (t + 1))
-            nc.tensor.matmul_mx(a_ps[t][:], lhsT=w_wd[:, cols].bitcast(E4M3), lhsT_scale=w_sd[:, cols],
-                                rhs=xt1_w[:].bitcast(E2M1), rhs_scale=xt1_s[:], start=True, stop=False)
-        for t in range(PACK):
-            cols = slice(P * t, P * (t + 1))
             nc.tensor.matmul_mx(g_ps[:, t, :], lhsT=wg_wd[:, cols].bitcast(E5M2), lhsT_scale=wg_sd[:, cols],
                                 rhs=xc_w[:].bitcast(E4M3), rhs_scale=xc_s, start=True, stop=True)
         for t in range(PACK):
             cols = slice(P * t, P * (t + 1))
+            nc.tensor.matmul_mx(a_ps[t][:], lhsT=w_wd[:, cols].bitcast(E4M3), lhsT_scale=w_sd[:, cols],
+                                rhs=xt1_w[:].bitcast(E2M1), rhs_scale=xt1_s[:], start=True, stop=False)
             nc.tensor.matmul_mx(a_ps[t][:], lhsT=w0_wd[:, cols].bitcast(E2M1), lhsT_scale=w0_sd[:, cols],
                                 rhs=xo2_w[:].bitcast(E4M3), rhs_scale=xo2_s[:], start=False, stop=True)
 
         gains = tile("gains", [P, PACK, 2], F32)
         nc.scalar.copy(gains[:], g_ps[:, :, 0:Q:64])
-        hid_g = tile("hid_g", [P, Q, PACK], BF16)
+        hid_g = tile("hid_g", [P, Q, PACK], BF16, "w0_w")
         nc.scalar.copy(hid_g[:], g_ps[:].rearrange("p t c -> p c t"))
         hid_h = tile("hid_h", [P, O, PACK], BF16)
         y3 = tile("y3", [P, PACK, O], F32)

@@ -106,8 +106,8 @@ def tile_list_ctxgroups_bank_further_pairweighed_kernel(
         load_quad(nc.sync, xt_p[:].bitcast(I32), xt_scales, 0, 2)
         load_quad(nc.sync, xt_p[:].bitcast(I32), xt_scales, 0, 3)
         wg_w = load_words(nc.sync, "wg_w", wg_words, U32)
-        xc_w = load_words(nc.sync, "xc_w", xc_words, U32)
         w0_w = load_words(nc.sync, "w0_w", w0_words, U16)
+        xc_w = load_words(nc.sync, "xc_w", xc_words, U32)
         load_quad(nc.sync, xo_p[:].bitcast(I32), xo_scales, 0, 0)
         load_quad(nc.sync, xo_p[:].bitcast(I32), xo_scales, 0, 1)
         load_quad(nc.sync, xo_p[:].bitcast(I32), xo_scales, 0, 2)
@@ -136,7 +136,7 @@ def tile_list_ctxgroups_bank_further_pairweighed_kernel(
         wg_sd = deal_scales(nc.vector, "wg_sd", W_p[:, 512:1024])
         xt1_s = gather("xt1_s", xt_p[:], l1, U8)
         w0_sd = deal_scales(nc.vector, "w0_sd", W_p[:, 1024:1536])
-        xo2_w = gather("xo2_w", xo_w[:], l2, U32)
+        xo2_w = gather("xo2_w", xo_w[:], l2, U32, "W_st")
         xo2_s = gather("xo2_s", xo_p[:], l2, U8)
         w_wd = deal_words(nc.scalar.copy, "w_wd", w_w, U32)
         wg_wd = deal_words(nc.scalar.copy, "wg_wd", wg_w, U32)

@@ -16,9 +16,18 @@ MAX = mybir.AluOpType.max
 
 P = 128
 PACK = 4
-T, J, R, Z, Q, O, D, N, U = 1024, 256, 512, 1024, 128, 128, 256, 256, 128
+QUADS = 4
+QUAD = P // QUADS
+LINE = 4
 K = 512
+T, Z = 1024, 1024
+J, R, Q, O, D, N, U = 256, 512, 128, 128, 256, 256, 128
+SECOND_CONTEXT = 64
+N_TILES = N // P
 FLOPS = 2 * K * (2 * R * J + R * Q + 2 * N * D)
+
+W_AT, WG_AT, W0_AT, XC_AT, FIRST_WIDTH = 0, R, 2 * R, 3 * R, 3 * R + Q
+WS_AT, WB_AT, SECOND_WIDTH = 0, N, 2 * N
 
 
 def tile_list_ctxgroups_bank_further_pairweighed_kernel(
@@ -34,116 +43,107 @@ def tile_list_ctxgroups_bank_further_pairweighed_kernel(
         def tile(name, shape, dtype, tag=None):
             return sb.tile(shape, dtype, name=name, tag=tag or name, align_bytes=64)
 
+        def zeroed_plane(name, width):
+            dst = tile(name, [P, width], U8)
+            nc.vector.memset(dst[:].bitcast(I32), 0)
+            return dst
+
         def load_list(name, src):
             dst = tile(name, list(src.shape), U16)
             nc.sync.dma_start(dst[:], src)
             return dst
 
-        def load_words(queue, name, src, dtype):
+        def load_words(name, src, dtype):
             rows = src[0] if src.ndim == 3 else src[0].rearrange("p c t -> p (c t)")
-            width = rows.shape[1] // (4 if dtype == U32 else 2)
-            dst = tile(name, [P, width], dtype)
-            queue.dma_start(dst[:].bitcast(I32), rows.bitcast(I32))
+            word_bytes = 4 if dtype == U32 else 2
+            dst = tile(name, [P, rows.shape[1] // word_bytes], dtype)
+            nc.sync.dma_start(dst[:].bitcast(I32), rows.bitcast(I32))
             return dst
 
-        def load_rows(queue, dst, src, col):
-            rows = src[0].bitcast(I32).rearrange("(q r) c -> r q c", r=4)
-            queue.dma_start(dst[:, :, col : col + rows.shape[2]], rows)
+        def stage_scales(queue, src, at):
+            rows = src[0].bitcast(I32).rearrange("(quad s) c -> s quad c", s=QUADS)
+            queue.dma_start(staged[:, :, at // 4 : at // 4 + rows.shape[2]], rows)
 
-        def load_half(queue, dst, src, col, h):
-            rows = src[0].bitcast(I32).rearrange("(b h r) c -> h r b c", b=2, h=2)
-            queue.dma_start(dst[32 * h : 32 * h + 4, :, col : col + rows.shape[3]], rows[h])
+        def load_scales(plane, src, at):
+            for quad in range(QUADS):
+                rows = src[0, QUADS * quad : QUADS * (quad + 1), :].bitcast(I32)
+                dst = plane[:].bitcast(I32)[QUAD * quad : QUAD * quad + QUADS, at // 4 : at // 4 + rows.shape[1]]
+                nc.sync.dma_start(dst, rows)
 
-        def load_quad(queue, dst, src, col, quad):
-            rows = src[0, 4 * quad : 4 * quad + 4, :].bitcast(I32)
-            queue.dma_start(dst[32 * quad : 32 * quad + 4, col : col + rows.shape[1]], rows)
-
-        so_t = tile("so_t", [P, 2], F32)
-        sp_t = tile("sp_t", [P, 2], F32)
-
-        def load_weight(queue, dst, src):
+        def load_feature_weights(dst, src):
             with nc.allow_non_contiguous_dma(reason="one weight a partition"):
-                queue.dma_start(dst[:], src.rearrange("(i p) o -> p (i o)", p=P))
+                nc.sync.dma_start(dst[:], src.rearrange("(i p) o -> p (i o)", p=P))
 
         def gather(name, window, offsets, dtype, tag=None):
             dst = tile(name, [P, J], dtype, tag)
-            nc.vector.tensor_copy(dst[:], window.indirect(offsets[:]))
+            nc.vector.tensor_copy(dst[:], window[:].indirect(offsets[:]))
             return dst
 
-        def deal_words(copy, name, src, dtype):
+        def deal_words(name, src, dtype):
             dst = tile(name, [P, R], dtype)
-            copy(
-                dst[:].rearrange("p (t b i) -> p b t i", t=PACK, i=4),
-                src[:].rearrange("p (b i t) -> p b t i", t=PACK, i=4),
+            nc.scalar.copy(
+                dst[:].rearrange("p (t b i) -> p b t i", t=PACK, i=LINE),
+                src[:].rearrange("p (b i t) -> p b t i", t=PACK, i=LINE),
             )
             return dst
 
-        def deal_scales(engine, name, src):
+        def deal_scales(engine, name, at):
             dst = tile(name, [P, R], U8)
-            engine.tensor_copy(dst[:].rearrange("p (t m) -> p t m", t=PACK), src.rearrange("p (m t) -> p t m", t=PACK))
+            engine.tensor_copy(
+                dst[:].rearrange("p (t m) -> p t m", t=PACK),
+                first_s[:, at : at + R].rearrange("p (m t) -> p t m", t=PACK),
+            )
             return dst
 
-        xt_p = tile("xt_p", [P, 1024], U8)
-        nc.vector.memset(xt_p[:].bitcast(I32), 0)
-        xo_p = tile("xo_p", [P, 1024], U8)
-        nc.vector.memset(xo_p[:].bitcast(I32), 0)
-        W_p = tile("W_p", [P, 1664], U8)
-        nc.vector.memset(W_p[:].bitcast(I32), 0)
-        W_st = tile("W_st", [4, 4, 416], I32)
-        B_p = tile("B_p", [P, 512], U8)
-        nc.vector.memset(B_p[:].bitcast(I32), 0)
+        so_t = tile("so_t", [P, N_TILES], F32)
+        sp_t = tile("sp_t", [P, N_TILES], F32)
+        xt_s = zeroed_plane("xt_p", T)
+        xo_s = zeroed_plane("xo_p", Z)
+        first_s = zeroed_plane("W_p", FIRST_WIDTH)
+        staged = tile("W_st", [QUADS, QUADS, FIRST_WIDTH // 4], I32)
+        second_s = zeroed_plane("B_p", SECOND_WIDTH)
+
         l1 = load_list("l1", offs)
-        load_rows(nc.scalar, W_st, w_scales, 0)
-        xt_w = load_words(nc.sync, "xt_w", xt_words, U16)
-        load_rows(nc.scalar, W_st, wg_scales, 128)
-        load_rows(nc.sync, W_st, xc_scales, 384)
-        load_rows(nc.scalar, W_st, w0_scales, 256)
+        stage_scales(nc.scalar, w_scales, W_AT)
+        xt_w = load_words("xt_w", xt_words, U16)
+        stage_scales(nc.scalar, wg_scales, WG_AT)
+        stage_scales(nc.sync, xc_scales, XC_AT)
+        stage_scales(nc.scalar, w0_scales, W0_AT)
         l2 = load_list("l2", offs2)
-        xo_w = load_words(nc.sync, "xo_w", xo_words, U32)
-        w_w = load_words(nc.sync, "w_w", w_words, U32)
-        load_quad(nc.sync, xt_p[:].bitcast(I32), xt_scales, 0, 0)
-        load_quad(nc.sync, xt_p[:].bitcast(I32), xt_scales, 0, 1)
-        load_quad(nc.sync, xt_p[:].bitcast(I32), xt_scales, 0, 2)
-        load_quad(nc.sync, xt_p[:].bitcast(I32), xt_scales, 0, 3)
-        wg_w = load_words(nc.sync, "wg_w", wg_words, U32)
-        w0_w = load_words(nc.sync, "w0_w", w0_words, U16)
-        xc_w = load_words(nc.sync, "xc_w", xc_words, U32)
-        load_quad(nc.sync, xo_p[:].bitcast(I32), xo_scales, 0, 0)
-        load_quad(nc.sync, xo_p[:].bitcast(I32), xo_scales, 0, 1)
-        load_quad(nc.sync, xo_p[:].bitcast(I32), xo_scales, 0, 2)
-        load_quad(nc.sync, xo_p[:].bitcast(I32), xo_scales, 0, 3)
+        xo_w = load_words("xo_w", xo_words, U32)
+        w_w = load_words("w_w", w_words, U32)
+        load_scales(xt_s, xt_scales, 0)
+        wg_w = load_words("wg_w", wg_words, U32)
+        w0_w = load_words("w0_w", w0_words, U16)
+        xc_w = load_words("xc_w", xc_words, U32)
+        load_scales(xo_s, xo_scales, 0)
         l5 = load_list("l5", offs5)
         l3 = load_list("l3", offs3)
         l4 = load_list("l4", offs4)
-        ws_w = load_words(nc.sync, "ws_w", ws_words, U32)
-        load_quad(nc.sync, B_p[:].bitcast(I32), ws_scales, 0, 0)
-        load_quad(nc.sync, B_p[:].bitcast(I32), ws_scales, 0, 1)
-        load_quad(nc.sync, B_p[:].bitcast(I32), ws_scales, 0, 2)
-        load_quad(nc.sync, B_p[:].bitcast(I32), ws_scales, 0, 3)
-        wb_w = load_words(nc.sync, "wb_w", wb_words, U16)
-        load_quad(nc.sync, B_p[:].bitcast(I32), wb_scales, 64, 0)
-        load_quad(nc.sync, B_p[:].bitcast(I32), wb_scales, 64, 1)
-        load_quad(nc.sync, B_p[:].bitcast(I32), wb_scales, 64, 2)
-        load_quad(nc.sync, B_p[:].bitcast(I32), wb_scales, 64, 3)
+        ws_w = load_words("ws_w", ws_words, U32)
+        load_scales(second_s, ws_scales, WS_AT)
+        wb_w = load_words("wb_w", wb_words, U16)
+        load_scales(second_s, wb_scales, WB_AT)
         l6 = load_list("l6", offs6)
         l7 = load_list("l7", offs7)
-        load_weight(nc.sync, so_t, so)
-        load_weight(nc.sync, sp_t, sp)
-        xt1_w = gather("xt1_w", xt_w[:], l1, U16)
-        for quad in range(4):
-            nc.vector.tensor_copy(W_p[32 * quad : 32 * quad + 4, :].bitcast(I32), W_st[:, quad, :])
-        w_sd = deal_scales(nc.vector, "w_sd", W_p[:, 0:512])
-        wg_sd = deal_scales(nc.vector, "wg_sd", W_p[:, 512:1024])
-        xt1_s = gather("xt1_s", xt_p[:], l1, U8)
-        w0_sd = deal_scales(nc.vector, "w0_sd", W_p[:, 1024:1536])
-        xo2_w = gather("xo2_w", xo_w[:], l2, U32, "W_st")
-        xo2_s = gather("xo2_s", xo_p[:], l2, U8)
-        w_wd = deal_words(nc.scalar.copy, "w_wd", w_w, U32)
-        wg_wd = deal_words(nc.scalar.copy, "wg_wd", wg_w, U32)
-        w0_wd = deal_words(nc.scalar.copy, "w0_wd", w0_w, U16)
-        xc_s = W_p[:, 1536:1664]
-        ws_s = B_p[:, 0:256]
-        wb_s = B_p[:, 256:512]
+        load_feature_weights(so_t, so)
+        load_feature_weights(sp_t, sp)
+
+        xt1_w = gather("xt1_w", xt_w, l1, U16)
+        for quad in range(QUADS):
+            nc.vector.tensor_copy(first_s[QUAD * quad : QUAD * quad + QUADS, :].bitcast(I32), staged[:, quad, :])
+        w_sd = deal_scales(nc.vector, "w_sd", W_AT)
+        wg_sd = deal_scales(nc.gpsimd, "wg_sd", WG_AT)
+        xt1_s = gather("xt1_s", xt_s, l1, U8)
+        w0_sd = deal_scales(nc.gpsimd, "w0_sd", W0_AT)
+        xo2_w = gather("xo2_w", xo_w, l2, U32, "W_st")
+        xo2_s = gather("xo2_s", xo_s, l2, U8)
+        w_wd = deal_words("w_wd", w_w, U32)
+        wg_wd = deal_words("wg_wd", wg_w, U32)
+        w0_wd = deal_words("w0_wd", w0_w, U16)
+        xc_s = first_s[:, XC_AT:FIRST_WIDTH]
+        ws_s = second_s[:, WS_AT:WB_AT]
+        wb_s = second_s[:, WB_AT:SECOND_WIDTH]
 
         a_ps = [ps.tile([P, J], F32, name="a_ps%d" % t) for t in range(PACK)]
         g_ps = ps.tile([P, PACK, Q], F32, name="g_ps")
@@ -159,7 +159,7 @@ def tile_list_ctxgroups_bank_further_pairweighed_kernel(
                                 rhs=xo2_w[:].bitcast(E4M3), rhs_scale=xo2_s[:], start=False, stop=True)
 
         gains = tile("gains", [P, PACK, 2], F32)
-        nc.scalar.copy(gains[:], g_ps[:, :, 0:Q:64])
+        nc.scalar.copy(gains[:], g_ps[:, :, 0:Q:SECOND_CONTEXT])
         hid_g = tile("hid_g", [P, Q, PACK], BF16, "w0_w")
         nc.scalar.copy(hid_g[:], g_ps[:].rearrange("p t c -> p c t"))
         hid_h = tile("hid_h", [P, O, PACK], BF16)
@@ -182,14 +182,15 @@ def tile_list_ctxgroups_bank_further_pairweighed_kernel(
         for t in range(PACK):
             nc.scalar.activation(y3[:, t, :], a_sb[t][:].indirect(l3[:]), COPY, scale=gains[:, t, 0:1])
             nc.scalar.activation(y4[:, t, :], a_sb[t][:].indirect(l4[:]), COPY, scale=gains[:, t, 1:2])
-        xt5_w = gather("xt5_w", xt_w[:], l5, U16)
+
+        xt5_w = gather("xt5_w", xt_w, l5, U16)
         hg_w, hg_s = quantise("hg", hid_g, "w0_wd")
-        xt5_s = gather("xt5_s", xt_p[:], l5, U8, "w0_sd")
+        xt5_s = gather("xt5_s", xt_s, l5, U8, "w0_sd")
         larger(slice(0, 2))
 
-        pg_ps = ps.tile([P, 2, Q], F32, name="pg_ps")
-        ph_ps = [ps.tile([P, O], F32, name="ph_ps%d" % i) for i in range(2)]
-        p_sb = [tile("p_sb%d" % i, [P, D], F32) for i in range(2)]
+        pg_ps = ps.tile([P, N_TILES, Q], F32, name="pg_ps")
+        ph_ps = [ps.tile([P, O], F32, name="ph_ps%d" % i) for i in range(N_TILES)]
+        p_sb = [tile("p_sb%d" % i, [P, D], F32) for i in range(N_TILES)]
 
         def short_way(dst, i, places):
             cols = slice(P * i, P * (i + 1))
@@ -201,20 +202,21 @@ def tile_list_ctxgroups_bank_further_pairweighed_kernel(
             nc.tensor.matmul_mx(dst, lhsT=wb_w[:, cols].bitcast(E2M1), lhsT_scale=wb_s[:, cols],
                                 rhs=codes[:].bitcast(E5M2), rhs_scale=scales[:], start=False, stop=True)
 
-        for i in range(2):
+        for i in range(N_TILES):
             short_way(pg_ps[:, i, :], i, slice(O, D))
             output_matrix(pg_ps[:, i, :], i, hg_w, hg_s)
-        for i in range(2):
+        for i in range(N_TILES):
             short_way(ph_ps[i][:], i, slice(0, O))
-        for i in range(2):
+        for i in range(N_TILES):
             nc.vector.tensor_copy(p_sb[i][:, O:D], pg_ps[:, i, :])
-        larger(slice(2, 4))
+        larger(slice(2, PACK))
         hh_w, hh_s = quantise("hh", hid_h)
-        for i in range(2):
+        for i in range(N_TILES):
             output_matrix(ph_ps[i][:], i, hh_w, hh_s)
-        for i in range(2):
+        for i in range(N_TILES):
             nc.vector.tensor_copy(p_sb[i][:, 0:O], ph_ps[i][:])
-        for i in range(2):
+
+        for i in range(N_TILES):
             y6 = tile("y6_%d" % i, [P, U], F32)
             y7 = tile("y7_%d" % i, [P, U], F32)
             res = tile("res%d" % i, [P, U], F32)

from contextlib import ExitStack

import concourse.mybir as mybir

F32 = mybir.dt.float32
BF16 = mybir.dt.bfloat16
I32 = mybir.dt.int32
U32 = mybir.dt.uint32
U16 = mybir.dt.uint16
U8 = mybir.dt.uint8
E4M3 = mybir.dt.float8_e4m3fn_x4
E5M2 = mybir.dt.float8_e5m2_x4
E2M1 = mybir.dt.float4_e2m1fn_x4
COPY = mybir.ActivationFunctionType.Copy
MAX = mybir.AluOpType.max

P = 128
PACK = 4
QUADS = 4
QUAD = P // QUADS
LINE = 4
K = 512
T, Z = 1024, 1024
J, R, Q, O, D, N, U = 256, 512, 128, 128, 256, 256, 128
SECOND_CONTEXT = 64
N_TILES = N // P
FLOPS = 2 * K * (2 * R * J + R * Q + 2 * N * D)

W_AT, WG_AT, W0_AT, XC_AT, FIRST_WIDTH = 0, R, 2 * R, 3 * R, 3 * R + Q
WS_AT, WB_AT, SECOND_WIDTH = 0, N, 2 * N


def tile_list_ctxgroups_bank_further_pairweighed_kernel(
    tc, xt_words, xt_scales, xo_words, xo_scales, w_words, w_scales, w0_words, w0_scales,
    xc_words, xc_scales, wg_words, wg_scales, wb_words, wb_scales, ws_words, ws_scales,
    so, sp, offs, offs2, offs3, offs4, offs5, offs6, offs7, out,
):
    nc = tc.nc
    with ExitStack() as ctx:
        sb = ctx.enter_context(tc.tile_pool(name="sb", bufs=1))
        ps = ctx.enter_context(tc.psum_pool(name="ps", bufs=1))

        def tile(name, shape, dtype, tag=None):
            return sb.tile(shape, dtype, name=name, tag=tag or name, align_bytes=64)

        def zeroed_plane(name, width):
            dst = tile(name, [P, width], U8)
            nc.vector.memset(dst[:].bitcast(I32), 0)
            return dst

        def load_list(name, src):
            dst = tile(name, list(src.shape), U16)
            nc.sync.dma_start(dst[:], src)
            return dst

        def load_words(name, src, dtype):
            rows = src[0] if src.ndim == 3 else src[0].rearrange("p c t -> p (c t)")
            word_bytes = 4 if dtype == U32 else 2
            dst = tile(name, [P, rows.shape[1] // word_bytes], dtype)
            nc.sync.dma_start(dst[:].bitcast(I32), rows.bitcast(I32))
            return dst

        def stage_scales(queue, src, at):
            rows = src[0].bitcast(I32).rearrange("(quad s) c -> s quad c", s=QUADS)
            queue.dma_start(staged[:, :, at // 4 : at // 4 + rows.shape[2]], rows)

        def load_scales(plane, src, at):
            for quad in range(QUADS):
                rows = src[0, QUADS * quad : QUADS * (quad + 1), :].bitcast(I32)
                dst = plane[:].bitcast(I32)[QUAD * quad : QUAD * quad + QUADS, at // 4 : at // 4 + rows.shape[1]]
                nc.sync.dma_start(dst, rows)

        def load_feature_weights(dst, src):
            with nc.allow_non_contiguous_dma(reason="one weight a partition"):
                nc.sync.dma_start(dst[:], src.rearrange("(i p) o -> p (i o)", p=P))

        def gather(name, window, offsets, dtype, tag=None):
            dst = tile(name, [P, J], dtype, tag)
            nc.vector.tensor_copy(dst[:], window[:].indirect(offsets[:]))
            return dst

        def deal_words(name, src, dtype):
            dst = tile(name, [P, R], dtype)
            nc.scalar.copy(
                dst[:].rearrange("p (t b i) -> p b t i", t=PACK, i=LINE),
                src[:].rearrange("p (b i t) -> p b t i", t=PACK, i=LINE),
            )
            return dst

        def deal_scales(engine, name, at):
            dst = tile(name, [P, R], U8)
            engine.tensor_copy(
                dst[:].rearrange("p (t m) -> p t m", t=PACK),
                first_s[:, at : at + R].rearrange("p (m t) -> p t m", t=PACK),
            )
            return dst

        so_t = tile("so_t", [P, N_TILES], F32)
        sp_t = tile("sp_t", [P, N_TILES], F32)
        xt_s = zeroed_plane("xt_p", T)
        xo_s = zeroed_plane("xo_p", Z)
        first_s = zeroed_plane("W_p", FIRST_WIDTH)
        staged = tile("W_st", [QUADS, QUADS, FIRST_WIDTH // 4], I32)
        second_s = zeroed_plane("B_p", SECOND_WIDTH)

        l1 = load_list("l1", offs)
        stage_scales(nc.scalar, w_scales, W_AT)
        xt_w = load_words("xt_w", xt_words, U16)
        stage_scales(nc.scalar, wg_scales, WG_AT)
        stage_scales(nc.sync, xc_scales, XC_AT)
        stage_scales(nc.scalar, w0_scales, W0_AT)
        l2 = load_list("l2", offs2)
        xo_w = load_words("xo_w", xo_words, U32)
        w_w = load_words("w_w", w_words, U32)
        load_scales(xt_s, xt_scales, 0)
        wg_w = load_words("wg_w", wg_words, U32)
        w0_w = load_words("w0_w", w0_words, U16)
        xc_w = load_words("xc_w", xc_words, U32)
        load_scales(xo_s, xo_scales, 0)
        l5 = load_list("l5", offs5)
        l3 = load_list("l3", offs3)
        l4 = load_list("l4", offs4)
        ws_w = load_words("ws_w", ws_words, U32)
        load_scales(second_s, ws_scales, WS_AT)
        wb_w = load_words("wb_w", wb_words, U16)
        load_scales(second_s, wb_scales, WB_AT)
        l6 = load_list("l6", offs6)
        l7 = load_list("l7", offs7)
        load_feature_weights(so_t, so)
        load_feature_weights(sp_t, sp)

        xt1_w = gather("xt1_w", xt_w, l1, U16)
        for quad in range(QUADS):
            nc.vector.tensor_copy(first_s[QUAD * quad : QUAD * quad + QUADS, :].bitcast(I32), staged[:, quad, :])
        w_sd = deal_scales(nc.vector, "w_sd", W_AT)
        wg_sd = deal_scales(nc.gpsimd, "wg_sd", WG_AT)
        xt1_s = gather("xt1_s", xt_s, l1, U8)
        w0_sd = deal_scales(nc.gpsimd, "w0_sd", W0_AT)
        xo2_w = gather("xo2_w", xo_w, l2, U32, "W_st")
        xo2_s = gather("xo2_s", xo_s, l2, U8)
        w_wd = deal_words("w_wd", w_w, U32)
        wg_wd = deal_words("wg_wd", wg_w, U32)
        w0_wd = deal_words("w0_wd", w0_w, U16)
        xc_s = first_s[:, XC_AT:FIRST_WIDTH]
        ws_s = second_s[:, WS_AT:WB_AT]
        wb_s = second_s[:, WB_AT:SECOND_WIDTH]

        a_ps = [ps.tile([P, J], F32, name="a_ps%d" % t) for t in range(PACK)]
        g_ps = ps.tile([P, PACK, Q], F32, name="g_ps")
        for t in range(PACK):
            cols = slice(P * t, P * (t + 1))
            nc.tensor.matmul_mx(g_ps[:, t, :], lhsT=wg_wd[:, cols].bitcast(E5M2), lhsT_scale=wg_sd[:, cols],
                                rhs=xc_w[:].bitcast(E4M3), rhs_scale=xc_s, start=True, stop=True)
        for t in range(PACK):
            cols = slice(P * t, P * (t + 1))
            nc.tensor.matmul_mx(a_ps[t][:], lhsT=w_wd[:, cols].bitcast(E4M3), lhsT_scale=w_sd[:, cols],
                                rhs=xt1_w[:].bitcast(E2M1), rhs_scale=xt1_s[:], start=True, stop=False)
            nc.tensor.matmul_mx(a_ps[t][:], lhsT=w0_wd[:, cols].bitcast(E2M1), lhsT_scale=w0_sd[:, cols],
                                rhs=xo2_w[:].bitcast(E4M3), rhs_scale=xo2_s[:], start=False, stop=True)

        gains = tile("gains", [P, PACK, 2], F32)
        nc.scalar.copy(gains[:], g_ps[:, :, 0:Q:SECOND_CONTEXT])
        hid_g = tile("hid_g", [P, Q, PACK], BF16, "w0_w")
        nc.scalar.copy(hid_g[:], g_ps[:].rearrange("p t c -> p c t"))
        hid_h = tile("hid_h", [P, O, PACK], BF16)
        y3 = tile("y3", [P, PACK, O], F32)
        y4 = tile("y4", [P, PACK, O], F32)
        a_sb = [tile("a_sb%d" % t, [P, J], F32) for t in range(PACK)]

        def quantise(name, src, tag=None):
            codes = tile(name + "_w", [P, P], U32, tag)
            scales = tile(name + "_s", [P, P], U8)
            nc.vector.quantize_mx(out=codes[:].bitcast(E5M2), scales=scales[:], in_=src[:].rearrange("p c t -> p (c t)"))
            return codes, scales

        def larger(pair):
            nc.vector.tensor_tensor(hid_h[:, :, pair], y3[:, pair, :].rearrange("p t c -> p c t"),
                                    y4[:, pair, :].rearrange("p t c -> p c t"), MAX)

        for t in range(PACK):
            nc.vector.tensor_copy(a_sb[t][:], a_ps[t][:])
        for t in range(PACK):
            nc.scalar.activation(y3[:, t, :], a_sb[t][:].indirect(l3[:]), COPY, scale=gains[:, t, 0:1])
            nc.scalar.activation(y4[:, t, :], a_sb[t][:].indirect(l4[:]), COPY, scale=gains[:, t, 1:2])

        xt5_w = gather("xt5_w", xt_w, l5, U16)
        hg_w, hg_s = quantise("hg", hid_g, "w0_wd")
        xt5_s = gather("xt5_s", xt_s, l5, U8, "w0_sd")
        larger(slice(0, 2))

        pg_ps = ps.tile([P, N_TILES, Q], F32, name="pg_ps")
        ph_ps = [ps.tile([P, O], F32, name="ph_ps%d" % i) for i in range(N_TILES)]
        p_sb = [tile("p_sb%d" % i, [P, D], F32) for i in range(N_TILES)]

        def short_way(dst, i, places):
            cols = slice(P * i, P * (i + 1))
            nc.tensor.matmul_mx(dst, lhsT=ws_w[:, cols].bitcast(E4M3), lhsT_scale=ws_s[:, cols],
                                rhs=xt5_w[:, places].bitcast(E2M1), rhs_scale=xt5_s[:, places], start=True, stop=False)

        def output_matrix(dst, i, codes, scales):
            cols = slice(P * i, P * (i + 1))
            nc.tensor.matmul_mx(dst, lhsT=wb_w[:, cols].bitcast(E2M1), lhsT_scale=wb_s[:, cols],
                                rhs=codes[:].bitcast(E5M2), rhs_scale=scales[:], start=False, stop=True)

        for i in range(N_TILES):
            short_way(pg_ps[:, i, :], i, slice(O, D))
            output_matrix(pg_ps[:, i, :], i, hg_w, hg_s)
        for i in range(N_TILES):
            short_way(ph_ps[i][:], i, slice(0, O))
        for i in range(N_TILES):
            nc.vector.tensor_copy(p_sb[i][:, O:D], pg_ps[:, i, :])
        larger(slice(2, PACK))
        hh_w, hh_s = quantise("hh", hid_h)
        for i in range(N_TILES):
            output_matrix(ph_ps[i][:], i, hh_w, hh_s)
        for i in range(N_TILES):
            nc.vector.tensor_copy(p_sb[i][:, 0:O], ph_ps[i][:])

        for i in range(N_TILES):
            y6 = tile("y6_%d" % i, [P, U], F32)
            y7 = tile("y7_%d" % i, [P, U], F32)
            res = tile("res%d" % i, [P, U], F32)
            nc.scalar.activation(y6[:], p_sb[i][:].indirect(l6[:]), COPY, scale=so_t[:, i : i + 1])
            nc.scalar.activation(y7[:], p_sb[i][:].indirect(l7[:]), COPY, scale=sp_t[:, i : i + 1])
            nc.vector.tensor_tensor(res[:], y6[:], y7[:], MAX)
            nc.sync.dma_start(out[P * i : P * (i + 1), :], res[:])
